import numpy as np
import ml_dtypes


def mxq(x, axis, fmt="e4m3"):
    dtype, down = {"e4m3": (ml_dtypes.float8_e4m3fn, 7), "e5m2": (ml_dtypes.float8_e5m2, 14)}[fmt]
    v = np.moveaxis(np.asarray(x, np.float32).astype(ml_dtypes.bfloat16).astype(np.float64), axis, -1)
    blocks = v.reshape(v.shape[:-1] + (-1, 32))
    amax = np.abs(blocks).max(-1, keepdims=True)
    byte = np.maximum(np.where(amax > 0, np.frexp(amax)[1] - 1 + 127, 0) - down, 1)
    scale = np.exp2(byte - 127.0)
    codes = (blocks / scale).astype(np.float32).astype(dtype).astype(np.float64)
    return np.moveaxis((codes * scale).reshape(v.shape), -1, axis)


WIDE = False


def mx_kscale(k):
    if not WIDE:
        return np.ones(k)
    levels = np.array([10, -10, 5, -5, 0])
    if k % 512:
        return np.exp2(np.random.permutation(np.resize(levels, k // 32))).repeat(32)
    a = np.empty((k // 512, 16))
    for p in range(k // 512):
        a[p, :8] = np.random.permutation(np.resize(levels, 8))
        for g in range(8):
            far = levels[np.abs(levels - a[p, g]) >= 10]
            a[p, g + 8] = far[np.random.randint(len(far))]
    return np.exp2(a.ravel()).repeat(32)


def f64(x):
    return np.asarray(x).astype(np.float64)


def striped(idx):
    return np.tile(idx.reshape(-1, 16).T, (8, 1)).astype(np.uint16)


def unstriped(offs):
    return offs[:16].T.reshape(-1).astype(np.int64)


E2M1 = np.array([0.0, 0.5, 1.0, 1.5, 2.0, 3.0, 4.0, 6.0, -0.0, -0.5, -1.0, -1.5, -2.0, -3.0, -4.0, -6.0])


def pack_weight(w, fmt):
    k, n = w.shape
    w = f64(np.asarray(w, np.float32).astype(ml_dtypes.bfloat16)).reshape(k // 32, 32, n)
    amax = np.abs(w).max(1)
    if fmt == "e4m3":
        byte = np.frexp(amax)[1] - 1 + 127 - 7
    else:
        mant, ex = np.frexp(amax / 6.0)
        byte = np.where(mant > 0.5, ex, ex - 1) + 127
    byte = np.clip(np.where(amax > 0, byte, 1), 1, 254)
    scaled = (w * np.exp2(127.0 - byte)[:, None, :]).reshape(k, n).astype(np.float32)
    by_word = np.ascontiguousarray(scaled.reshape(k // 512, 128, 4, n).transpose(0, 1, 3, 2))
    if fmt == "e4m3":
        words = by_word.astype(ml_dtypes.float8_e4m3fn).view(np.uint8)
    else:
        c = by_word.astype(ml_dtypes.float4_e2m1fn).view(np.uint8) & 0xF
        words = (c[..., 0::2] | (c[..., 1::2] << 4)).reshape(k // 512, 128, 2 * n)
    return np.ascontiguousarray(words), np.ascontiguousarray(byte.astype(np.uint8).reshape(k // 512, 16, n))


def unpack_weight(words, scales, fmt):
    g, _, n = scales.shape
    words = np.ascontiguousarray(words).reshape(g, 128, n, -1)
    if fmt == "e4m3":
        vals = words.view(ml_dtypes.float8_e4m3fn).astype(np.float64)
    else:
        nib = np.empty((g, 128, n, 4), np.uint8)
        nib[..., 0::2] = words & 0xF
        nib[..., 1::2] = words >> 4
        vals = E2M1[nib]
    vals = vals * np.repeat(np.exp2(scales.astype(np.float64) - 127.0), 8, axis=1)[..., None]
    return vals.transpose(0, 1, 3, 2).reshape(g * 512, n)


def relu(v):
    return np.maximum(v, 0.0)


K, T, E, C, H, N = 1536, 512, 4, 256, 512, 128


def by_expert(wq, xq):
    return np.concatenate([wq[e].T @ xq[:, e * C:(e + 1) * C] for e in range(E)], axis=1)


def setup_inputs():
    n = np.random.standard_normal
    s = mx_kscale(K)[:, None]
    u = mx_kscale(H)
    first = np.random.permutation(np.repeat(np.arange(E), T // E))
    second = (first + 1 + np.random.permutation(np.repeat(np.arange(E - 1), -(-T // (E - 1)))[:T])) % E
    while np.bincount(second, minlength=E).max() != T // E:
        load = np.bincount(second, minlength=E); hi, lo = int(load.argmax()), int(load.argmin())
        t = np.flatnonzero((second == hi) & (first != lo))[0]; second[t] = lo
    slot_token = np.empty(E * C, np.int64); pos = np.empty((2, T), np.int64); fill = np.zeros(E, np.int64)
    place = np.stack([np.random.permutation(C) for _ in range(E)])
    for r, deal in enumerate((first, second)):
        for t in np.random.permutation(T):
            e = deal[t]; j = e * C + place[e, fill[e]]; fill[e] += 1; slot_token[j] = t; pos[r, t] = j
    g = np.random.uniform(0.2, 0.8, T)
    x = pack_weight(n((K, T)) * s, "e4m3")
    return {
        "x_words": x[0],
        "x_scales": x[1],
        "w1": (n((E + 1, K, H)) / np.sqrt(K) / s[None]).astype(np.float32),
        "w3": (n((E + 1, K, H)) / np.sqrt(K) / s[None] * u[None, None, :]).astype(np.float32),
        "w2": (n((E + 1, H, N)) / np.sqrt(H) / u[None, :, None]).astype(np.float32),
        "gate": np.stack([np.tile(g, (N, 1)), np.tile(1.0 - g, (N, 1))]).astype(np.float32),
        "offs": striped(slot_token),
        "pos1": striped(pos[0]),
        "pos2": striped(pos[1]),
    }


def reference(x_words, x_scales, w1, w3, w2, gate, offs, pos1, pos2):
    idx = unstriped(offs)
    w1q, w3q, w2q = mxq(f64(w1), 1, "e4m3"), mxq(f64(w3), 1, "e4m3"), mxq(f64(w2), 1, "e4m3")
    xs = unpack_weight(x_words, x_scales, "e4m3")
    hs = relu(w1q[E].T @ xs) * (w3q[E].T @ xs)
    ys = w2q[E].T @ mxq(hs, 0, "e4m3")
    xq = unpack_weight(x_words, x_scales, "e4m3")[:, idx]
    h = relu(by_expert(w1q, xq))
    h = h * by_expert(w3q, xq)
    y = by_expert(w2q, mxq(h, 0, "e4m3"))
    return ys + f64(gate[0]) * y[:, unstriped(pos1)] + f64(gate[1]) * y[:, unstriped(pos2)]

@@ -1,0 +1,205 @@
+from contextlib import ExitStack
+
+import concourse.mybir as mybir
+from concourse.masks import make_identity
+
+K, T, E, C, H, N = 1536, 512, 4, 256, 512, 128
+FLOPS = 2 * (E * C + T) * H * (2 * K + N)
+
+F32 = mybir.dt.float32
+BF16 = mybir.dt.bfloat16
+I32 = mybir.dt.int32
+U32 = mybir.dt.uint32
+U16 = mybir.dt.uint16
+U8 = mybir.dt.uint8
+FP8X4 = mybir.dt.float8_e4m3fn_x4
+MULT = mybir.AluOpType.mult
+ADD = mybir.AluOpType.add
+RELU = mybir.ActivationFunctionType.Relu
+
+P = 128
+PACK = 4
+K_PASS = P * PACK
+PASSES = K // K_PASS
+SHARED = E
+SCALAR_COLS = 320
+
+
+def tile_moe_shr_glu_relu_kernel(
+    tc, x_words, x_scales, w1, w3, w2, gate, offs, pos1, pos2, out
+):
+    nc = tc.nc
+    with ExitStack() as ctx:
+        keep = ctx.enter_context(tc.tile_pool(name="keep", bufs=1))
+        raws = ctx.enter_context(tc.tile_pool(name="raws", bufs=11))
+        work = ctx.enter_context(tc.tile_pool(name="work", bufs=3))
+        codes = ctx.enter_context(tc.tile_pool(name="codes", bufs=12))
+        relus = ctx.enter_context(tc.tile_pool(name="relus", bufs=4))
+        acc_psum = ctx.enter_context(tc.psum_pool(name="acc_psum", bufs=4))
+        turn_psum = ctx.enter_context(tc.psum_pool(name="turn_psum", bufs=2))
+        y_psum = ctx.enter_context(tc.psum_pool(name="y_psum", bufs=2))
+
+        offs_sb = keep.tile([P, E * C // 16], U16, name="offs_sb")
+        nc.sync.dma_start(offs_sb[:], offs)
+        tok_words = keep.tile([P, PASSES * T], I32, name="tok_words", align_bytes=64)
+        nc.sync.dma_start(
+            out=tok_words[:].rearrange("p (o t) -> p o t", o=PASSES),
+            in_=x_words.rearrange("o p t r -> p o (t r)").bitcast(I32),
+        )
+        tok_scales = keep.tile([P, T], U8, name="tok_scales", align_bytes=64)
+        nc.vector.memset(tok_scales[:].bitcast(I32), 0)
+        for q in range(4):
+            nc.scalar.dma_start(
+                out=tok_scales[32 * q : 32 * q + 4 * PASSES, :].bitcast(I32),
+                in_=x_scales[:, 4 * q : 4 * q + 4, :].bitcast(I32),
+            )
+        ident = keep.tile([P, P], F32, name="ident")
+        make_identity(nc, ident[:])
+
+        y_slots = keep.tile([P, E * C], F32, name="y_slots")
+        routed_sum = keep.tile([P, T], F32, name="routed_sum")
+
+        def gather_tokens(e):
+            slots = offs_sb[:, e * C // 16 : (e + 1) * C // 16]
+            words = keep.tile([P, PASSES * C], U32, name="slot_words%d" % e, align_bytes=64)
+            scales = keep.tile([P, C], U8, name="slot_scales%d" % e, align_bytes=64)
+            nc.vector.tensor_copy(scales[:], tok_scales[:].indirect(slots))
+            for o in range(PASSES):
+                window = tok_words[:, o * T : (o + 1) * T].bitcast(U32)
+                nc.vector.tensor_copy(words[:, o * C : (o + 1) * C], window.indirect(slots))
+            return words, scales
+
+        def interleave(copy, grouped, raw, c0, c1):
+            copy(
+                out=grouped[:, PACK * c0 : PACK * c1].rearrange("p (c i j) -> p c j i", i=4, j=PACK),
+                in_=raw[:, :, c0:c1].rearrange("p j (c i) -> p c j i", i=4),
+            )
+
+        def quantize_pass(rows):
+            raw = raws.tile([P, PACK, H], F32, name="raw")
+            nc.sync.dma_start(out=raw[:], in_=rows.rearrange("(p j) c -> p j c", j=PACK))
+            grouped = work.tile([P, PACK * H], BF16, name="grouped", align_bytes=64)
+            interleave(nc.scalar.copy, grouped, raw, 0, SCALAR_COLS)
+            interleave(nc.vector.tensor_copy, grouped, raw, SCALAR_COLS, H)
+            w_codes = codes.tile([P, H], U32, name="w_codes", align_bytes=64)
+            w_scales = codes.tile([P, H], U8, name="w_scales", align_bytes=64)
+            nc.vector.quantize_mx(out=w_codes[:].bitcast(FP8X4), scales=w_scales[:], in_=grouped[:])
+            return w_codes, w_scales
+
+        def first_layer(w, words, scales, width):
+            blocks = width // P
+            banks = [acc_psum.tile([P, H], F32, name="acc") for b in range(blocks)]
+            for o in range(PASSES):
+                w_codes, w_scales = quantize_pass(w[o * K_PASS : (o + 1) * K_PASS, :])
+                for b in range(blocks):
+                    nc.tensor.matmul_mx(
+                        out=banks[b][:],
+                        lhsT=words[:, o * width + b * P : o * width + (b + 1) * P].bitcast(FP8X4),
+                        lhsT_scale=scales[4 * o : P, b * P : (b + 1) * P],
+                        rhs=w_codes[:].bitcast(FP8X4),
+                        rhs_scale=w_scales[:],
+                        start=(o == 0),
+                        stop=(o == PASSES - 1),
+                    )
+            return banks
+
+        def by_pairs(bank):
+            return bank[:].rearrange("s (p u e) -> s u p e", u=2, e=2)
+
+        def relu_out(bank):
+            act = relus.tile([P, H], F32, name="act")
+            nc.scalar.activation(act[:].rearrange("s (u p e) -> s u p e", u=2, e=2), by_pairs(bank), RELU)
+            return act
+
+        def quantize_w2(e):
+            raw = work.tile([P, PACK, N], F32, name="w2_raw")
+            nc.sync.dma_start(out=raw[:], in_=w2[e].rearrange("(p j) n -> p j n", j=PACK))
+            grouped = work.tile([P, PACK * N], BF16, name="w2_grouped", align_bytes=64)
+            interleave(nc.scalar.copy, grouped, raw, 0, N)
+            w_codes = work.tile([P, N], U32, name="w2_codes", align_bytes=64)
+            w_scales = work.tile([P, N], U8, name="w2_scales", align_bytes=64)
+            nc.vector.quantize_mx(out=w_codes[:].bitcast(FP8X4), scales=w_scales[:], in_=grouped[:])
+            return w_codes, w_scales
+
+        def second_layer(acts, banks, w2_codes, w2_scales):
+            width = len(banks) * P
+            turned = turn_psum.tile([P, 2, 2, P], F32, name="turned")
+            for b in range(len(banks)):
+                hidden = work.tile([P, H], BF16, name="hidden", align_bytes=64)
+                nc.vector.tensor_tensor(
+                    hidden[:].rearrange("s (u p e) -> s u p e", u=2, e=2),
+                    by_pairs(banks[b]),
+                    acts[b][:].rearrange("s (u p e) -> s u p e", u=2, e=2),
+                    MULT,
+                )
+                pairs = hidden[:].bitcast(F32)
+                for u in range(2):
+                    nc.tensor.transpose(turned[:, b, u, :], pairs[:, u * P : (u + 1) * P], ident[:])
+            grouped = work.tile([P, PACK * C], BF16, name="h_grouped", align_bytes=64)
+            nc.scalar.copy(
+                out=grouped[:, 0 : PACK * width].bitcast(F32).rearrange("p (b s u) -> p b s u", s=P, u=2),
+                in_=turned[:, 0 : len(banks), :, :].rearrange("p b u s -> p b s u"),
+            )
+            h_codes = work.tile([P, C], U32, name="h_codes", align_bytes=64)
+            h_scales = work.tile([P, C], U8, name="h_scales", align_bytes=64)
+            nc.vector.quantize_mx(
+                out=h_codes[:, 0:width].bitcast(FP8X4), scales=h_scales[:, 0:width], in_=grouped[:, 0 : PACK * width]
+            )
+            y_bank = y_psum.tile([P, C], F32, name="y_bank")
+            nc.tensor.matmul_mx(
+                out=y_bank[:, 0:width],
+                lhsT=w2_codes[:].bitcast(FP8X4),
+                lhsT_scale=w2_scales[:],
+                rhs=h_codes[:, 0:width].bitcast(FP8X4),
+                rhs_scale=h_scales[:, 0:width],
+                start=True,
+                stop=True,
+            )
+            return y_bank
+
+        def spread_gates():
+            column = keep.tile([P, 2, 4], F32, name="gate_column")
+            nc.sync.dma_start(out=column[:], in_=gate[:, 0, :].rearrange("r (p i) -> p r i", i=4))
+            gates = keep.tile([P, 2, T], F32, name="gates")
+            for r in range(2):
+                spread = turn_psum.tile([P, 4, P], F32, name="turned")
+                for i in range(4):
+                    nc.tensor.transpose(spread[:, i, :], column[:, r, i : i + 1].to_broadcast([P, P]), ident[:])
+                nc.scalar.copy(
+                    out=gates[:, r, :].rearrange("n (p i) -> n p i", i=4),
+                    in_=spread[:].rearrange("n i p -> n p i"),
+                )
+            return gates
+
+        pos_sb = []
+        gates = None
+        for e in range(E):
+            words, scales = gather_tokens(e)
+            acts = [relu_out(bank) for bank in first_layer(w1[e], words, scales, C)]
+            w2_codes, w2_scales = quantize_w2(e)
+            if e == 1:
+                for name, pos in (("pos1_sb", pos1), ("pos2_sb", pos2)):
+                    pos_tile = keep.tile([P, T // 16], U16, name=name)
+                    nc.sync.dma_start(pos_tile[:], pos)
+                    pos_sb.append(pos_tile)
+                gates = spread_gates()
+            banks = first_layer(w3[e], words, scales, C)
+            y_bank = second_layer(acts, banks, w2_codes, w2_scales)
+            nc.scalar.copy(out=y_slots[:, e * C : (e + 1) * C], in_=y_bank[:])
+
+        picked = []
+        for r in range(2):
+            product = keep.tile([P, T], F32, name="picked%d" % r)
+            nc.vector.tensor_tensor(product[:], y_slots[:].indirect(pos_sb[r][:]), gates[:, r, :], MULT)
+            picked.append(product)
+        nc.vector.tensor_tensor(routed_sum[:], picked[0][:], picked[1][:], ADD)
+
+        acts = [relu_out(bank) for bank in first_layer(w1[SHARED], tok_words, tok_scales, T)]
+        banks = first_layer(w3[SHARED], tok_words, tok_scales, T)
+        w2_codes, w2_scales = quantize_w2(SHARED)
+        for b in range(T // P):
+            cols = slice(b * P, (b + 1) * P)
+            y_bank = second_layer(acts[b : b + 1], banks[b : b + 1], w2_codes, w2_scales)
+            result = keep.tile([P, P], F32, name="result%d" % b)
+            nc.vector.tensor_tensor(result[:], y_bank[:, 0:P], routed_sum[:, cols], ADD)
+            nc.sync.dma_start(out=out[:, cols], in_=result[:])

@@ -22,7 +22,16 @@ PACK = 4
 K_PASS = P * PACK
 PASSES = K // K_PASS
 SHARED = E
-SCALAR_COLS = 320
+STEPS = 2 * PASSES
+TAIL_SCALAR_COLS = 176
+RAW_DEPTH = 16
+LAST_TURN = 25
+TURN_ANCHOR = True
+GATE_STEP = 5
+SLOT_DEPTH = 2
+VECTOR_EXTRA = (28,)
+SCALAR_EXTRA = ()
+SHARED_ANCHOR = 27
 
 
 def tile_moe_shr_glu_relu_kernel(
@@ -31,14 +40,30 @@ def tile_moe_shr_glu_relu_kernel(
     nc = tc.nc
     with ExitStack() as ctx:
         keep = ctx.enter_context(tc.tile_pool(name="keep", bufs=1))
-        raws = ctx.enter_context(tc.tile_pool(name="raws", bufs=11))
-        work = ctx.enter_context(tc.tile_pool(name="work", bufs=3))
-        codes = ctx.enter_context(tc.tile_pool(name="codes", bufs=12))
-        relus = ctx.enter_context(tc.tile_pool(name="relus", bufs=4))
-        acc_psum = ctx.enter_context(tc.psum_pool(name="acc_psum", bufs=4))
-        turn_psum = ctx.enter_context(tc.psum_pool(name="turn_psum", bufs=2))
-        y_psum = ctx.enter_context(tc.psum_pool(name="y_psum", bufs=2))
+        rings = ctx.enter_context(tc.tile_pool(name="rings", bufs=1))
+        psum = ctx.enter_context(tc.psum_pool(name="psum", bufs=1))
+        taken = {}
 
+        def ring(pool, name, depth, shape, dtype):
+            taken[name] = taken.get(name, 0) + 1
+            return pool.tile(shape, dtype, name="%s_%d" % (name, taken[name] % depth), align_bytes=64)
+
+        def bank(index, shape):
+            return psum.tile(shape, F32, name="bank%d" % index)
+
+        free = list(range(RAW_DEPTH))
+        held = {}
+
+        def stage(key, width):
+            held[key] = free[0]
+            free.remove(held[key])
+            return rings.tile([P, PACK, width], F32, name="raw%d" % held[key], align_bytes=64)
+
+        def release(key):
+            free.append(held[key])
+
+        first = stage(0, H)
+        nc.sync.dma_start(out=first[:], in_=w1[0, 0:K_PASS, :].rearrange("(p j) c -> p j c", j=PACK))
         offs_sb = keep.tile([P, E * C // 16], U16, name="offs_sb")
         nc.sync.dma_start(offs_sb[:], offs)
         tok_words = keep.tile([P, PASSES * T], I32, name="tok_words", align_bytes=64)
@@ -47,9 +72,9 @@ def tile_moe_shr_glu_relu_kernel(
             in_=x_words.rearrange("o p t r -> p o (t r)").bitcast(I32),
         )
         tok_scales = keep.tile([P, T], U8, name="tok_scales", align_bytes=64)
-        nc.vector.memset(tok_scales[:].bitcast(I32), 0)
+        nc.gpsimd.memset(tok_scales[:].bitcast(I32), 0)
         for q in range(4):
-            nc.scalar.dma_start(
+            nc.sync.dma_start(
                 out=tok_scales[32 * q : 32 * q + 4 * PASSES, :].bitcast(I32),
                 in_=x_scales[:, 4 * q : 4 * q + 4, :].bitcast(I32),
             )
@@ -61,8 +86,8 @@ def tile_moe_shr_glu_relu_kernel(
 
         def gather_tokens(e):
             slots = offs_sb[:, e * C // 16 : (e + 1) * C // 16]
-            words = keep.tile([P, PASSES * C], U32, name="slot_words%d" % e, align_bytes=64)
-            scales = keep.tile([P, C], U8, name="slot_scales%d" % e, align_bytes=64)
+            words = ring(rings, "slot_words", SLOT_DEPTH, [P, PASSES * C], U32)
+            scales = ring(rings, "slot_scales", SLOT_DEPTH, [P, C], U8)
             nc.vector.tensor_copy(scales[:], tok_scales[:].indirect(slots))
             for o in range(PASSES):
                 window = tok_words[:, o * T : (o + 1) * T].bitcast(U32)
@@ -75,83 +100,90 @@ def tile_moe_shr_glu_relu_kernel(
                 in_=raw[:, :, c0:c1].rearrange("p j (c i) -> p c j i", i=4),
             )
 
-        def quantize_pass(rows):
-            raw = raws.tile([P, PACK, H], F32, name="raw")
+        def load_pass(s):
+            e, m, o = s // STEPS, s // PASSES % 2, s % PASSES
+            raw = stage(s, H)
+            rows = (w1, w3)[m][e, o * K_PASS : (o + 1) * K_PASS, :]
             nc.sync.dma_start(out=raw[:], in_=rows.rearrange("(p j) c -> p j c", j=PACK))
-            grouped = work.tile([P, PACK * H], BF16, name="grouped", align_bytes=64)
-            interleave(nc.scalar.copy, grouped, raw, 0, SCALAR_COLS)
-            interleave(nc.vector.tensor_copy, grouped, raw, SCALAR_COLS, H)
-            w_codes = codes.tile([P, H], U32, name="w_codes", align_bytes=64)
-            w_scales = codes.tile([P, H], U8, name="w_scales", align_bytes=64)
-            nc.vector.quantize_mx(out=w_codes[:].bitcast(FP8X4), scales=w_scales[:], in_=grouped[:])
-            return w_codes, w_scales
+            return raw
 
-        def first_layer(w, words, scales, width):
-            blocks = width // P
-            banks = [acc_psum.tile([P, H], F32, name="acc") for b in range(blocks)]
-            for o in range(PASSES):
-                w_codes, w_scales = quantize_pass(w[o * K_PASS : (o + 1) * K_PASS, :])
-                for b in range(blocks):
-                    nc.tensor.matmul_mx(
-                        out=banks[b][:],
-                        lhsT=words[:, o * width + b * P : o * width + (b + 1) * P].bitcast(FP8X4),
-                        lhsT_scale=scales[4 * o : P, b * P : (b + 1) * P],
-                        rhs=w_codes[:].bitcast(FP8X4),
-                        rhs_scale=w_scales[:],
-                        start=(o == 0),
-                        stop=(o == PASSES - 1),
-                    )
-            return banks
+        def cast_pass(raw, scalar_cols):
+            grouped = ring(rings, "grouped", 4, [P, PACK * H], BF16)
+            if scalar_cols > 0:
+                interleave(nc.scalar.copy, grouped, raw, 0, scalar_cols)
+            if scalar_cols < H:
+                interleave(nc.vector.tensor_copy, grouped, raw, scalar_cols, H)
+            return grouped
+
+        def multiply_pass(grouped, o, banks, words, scales):
+            width = len(banks) * P
+            w_codes = ring(rings, "w_codes", 6, [P, H], U32)
+            w_scales = ring(rings, "w_scales", 6, [P, H], U8)
+            nc.vector.quantize_mx(out=w_codes[:].bitcast(FP8X4), scales=w_scales[:], in_=grouped[:])
+            for b in range(len(banks)):
+                nc.tensor.matmul_mx(
+                    out=banks[b][:],
+                    lhsT=words[:, o * width + b * P : o * width + (b + 1) * P].bitcast(FP8X4),
+                    lhsT_scale=scales[4 * o : P, b * P : (b + 1) * P],
+                    rhs=w_codes[:].bitcast(FP8X4),
+                    rhs_scale=w_scales[:],
+                    start=(o == 0),
+                    stop=(o == PASSES - 1),
+                )
 
         def by_pairs(bank):
             return bank[:].rearrange("s (p u e) -> s u p e", u=2, e=2)
 
-        def relu_out(bank):
-            act = relus.tile([P, H], F32, name="act")
-            nc.scalar.activation(act[:].rearrange("s (u p e) -> s u p e", u=2, e=2), by_pairs(bank), RELU)
-            return act
+        def relu_out(bank, act):
+            nc.scalar.activation(act.rearrange("s (u p e) -> s u p e", u=2, e=2), by_pairs(bank), RELU)
 
-        def quantize_w2(e):
-            raw = work.tile([P, PACK, N], F32, name="w2_raw")
+        def load_w2(e):
+            raw = stage("w2", N)
             nc.sync.dma_start(out=raw[:], in_=w2[e].rearrange("(p j) n -> p j n", j=PACK))
-            grouped = work.tile([P, PACK * N], BF16, name="w2_grouped", align_bytes=64)
-            interleave(nc.scalar.copy, grouped, raw, 0, N)
-            w_codes = work.tile([P, N], U32, name="w2_codes", align_bytes=64)
-            w_scales = work.tile([P, N], U8, name="w2_scales", align_bytes=64)
-            nc.vector.quantize_mx(out=w_codes[:].bitcast(FP8X4), scales=w_scales[:], in_=grouped[:])
-            return w_codes, w_scales
+            return raw
 
-        def second_layer(acts, banks, w2_codes, w2_scales):
-            width = len(banks) * P
-            turned = turn_psum.tile([P, 2, 2, P], F32, name="turned")
+        def cast_w2(raw):
+            grouped = ring(rings, "w2_grouped", 4, [P, PACK * N], BF16)
+            interleave(nc.vector.tensor_copy, grouped, raw, 0, N)
+            return grouped[:]
+
+        def quantize(grouped, width, name):
+            q_codes = ring(rings, name + "_codes", 4, [P, width], U32)
+            q_scales = ring(rings, name + "_scales", 4, [P, width], U8)
+            nc.vector.quantize_mx(out=q_codes[:].bitcast(FP8X4), scales=q_scales[:], in_=grouped)
+            return q_codes, q_scales
+
+        def gate_and_turn(acts, banks, turn_bank):
+            turned = bank(turn_bank, [P, 2, 2, P])
             for b in range(len(banks)):
-                hidden = work.tile([P, H], BF16, name="hidden", align_bytes=64)
+                hidden = ring(rings, "hidden", 4, [P, H], BF16)
                 nc.vector.tensor_tensor(
                     hidden[:].rearrange("s (u p e) -> s u p e", u=2, e=2),
                     by_pairs(banks[b]),
-                    acts[b][:].rearrange("s (u p e) -> s u p e", u=2, e=2),
+                    acts[b].rearrange("s (u p e) -> s u p e", u=2, e=2),
                     MULT,
                 )
                 pairs = hidden[:].bitcast(F32)
                 for u in range(2):
                     nc.tensor.transpose(turned[:, b, u, :], pairs[:, u * P : (u + 1) * P], ident[:])
-            grouped = work.tile([P, PACK * C], BF16, name="h_grouped", align_bytes=64)
+            return turned
+
+        def group_hidden(turned, blocks, pairs):
             nc.scalar.copy(
-                out=grouped[:, 0 : PACK * width].bitcast(F32).rearrange("p (b s u) -> p b s u", s=P, u=2),
-                in_=turned[:, 0 : len(banks), :, :].rearrange("p b u s -> p b s u"),
+                out=pairs.rearrange("p (b s u) -> p b s u", s=P, u=2),
+                in_=turned[:, 0:blocks, :, :].rearrange("p b u s -> p b s u"),
             )
-            h_codes = work.tile([P, C], U32, name="h_codes", align_bytes=64)
-            h_scales = work.tile([P, C], U8, name="h_scales", align_bytes=64)
-            nc.vector.quantize_mx(
-                out=h_codes[:, 0:width].bitcast(FP8X4), scales=h_scales[:, 0:width], in_=grouped[:, 0 : PACK * width]
-            )
-            y_bank = y_psum.tile([P, C], F32, name="y_bank")
+            return pairs.bitcast(BF16)
+
+        def second_layer(h_q, width, w2_q, y_index):
+            h_codes, h_scales = h_q
+            y_bank = bank(y_index, [P, C])
             nc.tensor.matmul_mx(
                 out=y_bank[:, 0:width],
-                lhsT=w2_codes[:].bitcast(FP8X4),
-                lhsT_scale=w2_scales[:],
-                rhs=h_codes[:, 0:width].bitcast(FP8X4),
-                rhs_scale=h_scales[:, 0:width],
+                lhsT=w2_q[0][:].bitcast(FP8X4),
+                lhsT_scale=w2_q[1][:],
+                rhs=h_codes[:].bitcast(FP8X4),
+                rhs_scale=h_scales[:],
                 start=True,
                 stop=True,
             )
@@ -162,7 +194,7 @@ def tile_moe_shr_glu_relu_kernel(
             nc.sync.dma_start(out=column[:], in_=gate[:, 0, :].rearrange("r (p i) -> p r i", i=4))
             gates = keep.tile([P, 2, T], F32, name="gates")
             for r in range(2):
-                spread = turn_psum.tile([P, 4, P], F32, name="turned")
+                spread = bank(2 + r, [P, 4, P])
                 for i in range(4):
                     nc.tensor.transpose(spread[:, i, :], column[:, r, i : i + 1].to_broadcast([P, P]), ident[:])
                 nc.scalar.copy(
@@ -171,35 +203,86 @@ def tile_moe_shr_glu_relu_kernel(
                 )
             return gates
 
-        pos_sb = []
-        gates = None
-        for e in range(E):
-            words, scales = gather_tokens(e)
-            acts = [relu_out(bank) for bank in first_layer(w1[e], words, scales, C)]
-            w2_codes, w2_scales = quantize_w2(e)
-            if e == 1:
-                for name, pos in (("pos1_sb", pos1), ("pos2_sb", pos2)):
-                    pos_tile = keep.tile([P, T // 16], U16, name=name)
-                    nc.sync.dma_start(pos_tile[:], pos)
-                    pos_sb.append(pos_tile)
-                gates = spread_gates()
-            banks = first_layer(w3[e], words, scales, C)
-            y_bank = second_layer(acts, banks, w2_codes, w2_scales)
+        def load_list(pos, name):
+            pos_tile = keep.tile([P, T // 16], U16, name=name)
+            nc.sync.dma_start(pos_tile[:], pos)
+            return pos_tile
+
+        def pick(pos_tile, gates_row, name):
+            product = keep.tile([P, T], F32, name=name)
+            nc.vector.tensor_tensor(product[:], y_slots[:].indirect(pos_tile[:]), gates_row, MULT)
+            return product
+
+        tokens = {0: gather_tokens(0), SHARED: (tok_words, tok_scales)}
+        raws, grouped, banks, acts, w2_q, st = {}, {}, {}, {}, {}, {}
+        last = STEPS * (E + 1) - 1
+
+        def store_slots(e):
+            y_bank = second_layer(st["h_q"], C, w2_q[e], 4)
             nc.scalar.copy(out=y_slots[:, e * C : (e + 1) * C], in_=y_bank[:])
 
-        picked = []
-        for r in range(2):
-            product = keep.tile([P, T], F32, name="picked%d" % r)
-            nc.vector.tensor_tensor(product[:], y_slots[:].indirect(pos_sb[r][:]), gates[:, r, :], MULT)
-            picked.append(product)
-        nc.vector.tensor_tensor(routed_sum[:], picked[0][:], picked[1][:], ADD)
+        for s in range(last + 2):
+            e, k = divmod(s, STEPS)
+            if s <= last:
+                raws[s] = first if s == 0 else load_pass(s)
+                on_vector = (s % PASSES == PASSES - 1 or s in VECTOR_EXTRA) and s not in SCALAR_EXTRA
+                share = TAIL_SCALAR_COLS if s == last else (0 if on_vector else H)
+                grouped[s] = cast_pass(raws[s], share)
+            if s >= 1:
+                pe, pm, po = (s - 1) // STEPS, (s - 1) // PASSES % 2, (s - 1) % PASSES
+                if po == 0:
+                    blocks = (T if pe == SHARED else C) // P
+                    base = 4 * pm if pe == SHARED else 4 + 2 * pm
+                    banks[pe, pm] = [bank(base + b, [P, H]) for b in range(blocks)]
+                multiply_pass(grouped[s - 1], po, banks[pe, pm], tokens[pe][0], tokens[pe][1])
+            if k == 0 and 1 <= e <= E:
+                st["turned"] = gate_and_turn(acts[e - 1], banks[e - 1, 1], 0 if e < E else 5)
+                if e < E:
+                    tokens[e] = gather_tokens(e)
+            if (k == 1 and 1 <= e < E) or s == LAST_TURN:
+                st["h_q"] = quantize(group_hidden(st["turned"], C // P, raws[s if TURN_ANCHOR or e < E else 13][:, 0, :]), C, "h")
+                if e == E:
+                    store_slots(e - 1)
+            if k == 3 and e < E:
+                st["w2_raw"] = load_w2(e)
+            if k == 4 and e < E:
+                w2_q[e] = quantize(cast_w2(st["w2_raw"]), N, "w2")
+                release("w2")
+                release(s - 1)
+                acts[e] = [raws[s][:, b, :] for b in range(C // P)]
+                for b in range(C // P):
+                    relu_out(banks[e, 0][b], acts[e][b])
+                if e >= 1:
+                    store_slots(e - 1)
+            if k == 3 and e == E:
+                home = raws[SHARED_ANCHOR] if SHARED_ANCHOR >= 0 else raws[7]
+                acts[e] = [home[:, b, :] for b in range(T // P)]
+                for b in range(T // P):
+                    relu_out(banks[e, 0][b], acts[e][b])
+            if s == GATE_STEP:
+                gates = spread_gates()
+            if s == 8:
+                pos_sb = [load_list(pos1, "pos1_sb"), load_list(pos2, "pos2_sb")]
+            if s <= last and not (e < E and (k in (3, 4) or (k == 1 and e >= 1))):
+                release(s)
+            if s == STEPS * E + 3:
+                picked = [pick(pos_sb[0], gates[:, 0, :], "picked0")]
+            if s == STEPS * E + 4:
+                picked.append(pick(pos_sb[1], gates[:, 1, :], "picked1"))
+                nc.vector.tensor_tensor(routed_sum[:], picked[0][:], picked[1][:], ADD)
+            if s == last:
+                st["w2_raw"] = load_w2(SHARED)
 
-        acts = [relu_out(bank) for bank in first_layer(w1[SHARED], tok_words, tok_scales, T)]
-        banks = first_layer(w3[SHARED], tok_words, tok_scales, T)
-        w2_codes, w2_scales = quantize_w2(SHARED)
-        for b in range(T // P):
-            cols = slice(b * P, (b + 1) * P)
-            y_bank = second_layer(acts[b : b + 1], banks[b : b + 1], w2_codes, w2_scales)
-            result = keep.tile([P, P], F32, name="result%d" % b)
-            nc.vector.tensor_tensor(result[:], y_bank[:, 0:P], routed_sum[:, cols], ADD)
-            nc.sync.dma_start(out=out[:, cols], in_=result[:])
+        w2_q[SHARED] = quantize(cast_w2(st["w2_raw"]), N, "w2")
+        h_grouped, y_banks = {}, {}
+        for b in range(T // P + 2):
+            if b < T // P:
+                turned = gate_and_turn(acts[SHARED][b : b + 1], banks[SHARED, 1][b : b + 1], b)
+                h_grouped[b] = group_hidden(turned, 1, ring(rings, "h_pairs", 4, [P, 2 * P], F32)[:])
+            if 1 <= b <= T // P:
+                y_banks[b - 1] = second_layer(quantize(h_grouped[b - 1], P, "h"), P, w2_q[SHARED], 4 + b - 1)
+            if b >= 2:
+                cols = slice((b - 2) * P, (b - 1) * P)
+                result = keep.tile([P, P], F32, name="result%d" % (b - 2))
+                nc.vector.tensor_tensor(result[:], y_banks[b - 2][:, 0:P], routed_sum[:, cols], ADD)
+                nc.sync.dma_start(out=out[:, cols], in_=result[:])

@@ -23,14 +23,19 @@ K_PASS = P * PACK
 PASSES = K // K_PASS
 SHARED = E
 STEPS = 2 * PASSES
-TAIL_SCALAR_COLS = 176
+TAIL_SCALAR_COLS = 256
 RAW_DEPTH = 16
-LAST_TURN = 25
+SHARES = {}
+PICK0 = 19
+PICK1 = 26
+Y_ON_V = True
+PICK_STEP = 27
+LAST_TURN = 24
 TURN_ANCHOR = True
 GATE_STEP = 5
 SLOT_DEPTH = 2
-VECTOR_EXTRA = (28,)
-SCALAR_EXTRA = ()
+VECTOR_EXTRA = (25, 28)
+SCALAR_EXTRA = (26,)
 SHARED_ANCHOR = 27
 
 
@@ -142,9 +147,9 @@ def tile_moe_shr_glu_relu_kernel(
             nc.sync.dma_start(out=raw[:], in_=w2[e].rearrange("(p j) n -> p j n", j=PACK))
             return raw
 
-        def cast_w2(raw):
+        def cast_w2(raw, copy):
             grouped = ring(rings, "w2_grouped", 4, [P, PACK * N], BF16)
-            interleave(nc.vector.tensor_copy, grouped, raw, 0, N)
+            interleave(copy, grouped, raw, 0, N)
             return grouped[:]
 
         def quantize(grouped, width, name):
@@ -208,9 +213,8 @@ def tile_moe_shr_glu_relu_kernel(
             nc.sync.dma_start(pos_tile[:], pos)
             return pos_tile
 
-        def pick(pos_tile, gates_row, name):
-            product = keep.tile([P, T], F32, name=name)
-            nc.vector.tensor_tensor(product[:], y_slots[:].indirect(pos_tile[:]), gates_row, MULT)
+        def pick(pos_tile, gates_row, product):
+            nc.vector.tensor_tensor(product, y_slots[:].indirect(pos_tile[:]), gates_row, MULT)
             return product
 
         tokens = {0: gather_tokens(0), SHARED: (tok_words, tok_scales)}
@@ -219,14 +223,14 @@ def tile_moe_shr_glu_relu_kernel(
 
         def store_slots(e):
             y_bank = second_layer(st["h_q"], C, w2_q[e], 4)
-            nc.scalar.copy(out=y_slots[:, e * C : (e + 1) * C], in_=y_bank[:])
+            (nc.vector.tensor_copy if e == E - 1 and Y_ON_V else nc.scalar.copy)(out=y_slots[:, e * C : (e + 1) * C], in_=y_bank[:])
 
         for s in range(last + 2):
             e, k = divmod(s, STEPS)
             if s <= last:
                 raws[s] = first if s == 0 else load_pass(s)
                 on_vector = (s % PASSES == PASSES - 1 or s in VECTOR_EXTRA) and s not in SCALAR_EXTRA
-                share = TAIL_SCALAR_COLS if s == last else (0 if on_vector else H)
+                share = SHARES.get(s, TAIL_SCALAR_COLS if s == last else (0 if on_vector else H))
                 grouped[s] = cast_pass(raws[s], share)
             if s >= 1:
                 pe, pm, po = (s - 1) // STEPS, (s - 1) // PASSES % 2, (s - 1) % PASSES
@@ -246,15 +250,15 @@ def tile_moe_shr_glu_relu_kernel(
             if k == 3 and e < E:
                 st["w2_raw"] = load_w2(e)
             if k == 4 and e < E:
-                w2_q[e] = quantize(cast_w2(st["w2_raw"]), N, "w2")
+                w2_q[e] = quantize(cast_w2(st["w2_raw"], nc.vector.tensor_copy), N, "w2")
                 release("w2")
                 release(s - 1)
-                acts[e] = [raws[s][:, b, :] for b in range(C // P)]
+                acts[e] = [raws[s - 1 if s in VECTOR_EXTRA else s][:, b, :] for b in range(C // P)]
                 for b in range(C // P):
                     relu_out(banks[e, 0][b], acts[e][b])
                 if e >= 1:
                     store_slots(e - 1)
-            if k == 3 and e == E:
+            if s == max(SHARED_ANCHOR, 27):
                 home = raws[SHARED_ANCHOR] if SHARED_ANCHOR >= 0 else raws[7]
                 acts[e] = [home[:, b, :] for b in range(T // P)]
                 for b in range(T // P):
@@ -265,24 +269,21 @@ def tile_moe_shr_glu_relu_kernel(
                 pos_sb = [load_list(pos1, "pos1_sb"), load_list(pos2, "pos2_sb")]
             if s <= last and not (e < E and (k in (3, 4) or (k == 1 and e >= 1))):
                 release(s)
-            if s == STEPS * E + 3:
-                picked = [pick(pos_sb[0], gates[:, 0, :], "picked0")]
-            if s == STEPS * E + 4:
-                picked.append(pick(pos_sb[1], gates[:, 1, :], "picked1"))
-                nc.vector.tensor_tensor(routed_sum[:], picked[0][:], picked[1][:], ADD)
+            if s == PICK_STEP:
+                picked = [pick(pos_sb[0], gates[:, 0, :], raws[PICK0][:, 1, :])]
+            if s == PICK_STEP:
+                picked.append(pick(pos_sb[1], gates[:, 1, :], raws[PICK1][:, 2, :]))
+                nc.vector.tensor_tensor(routed_sum[:], picked[0], picked[1], ADD)
             if s == last:
                 st["w2_raw"] = load_w2(SHARED)
 
-        w2_q[SHARED] = quantize(cast_w2(st["w2_raw"]), N, "w2")
-        h_grouped, y_banks = {}, {}
-        for b in range(T // P + 2):
-            if b < T // P:
-                turned = gate_and_turn(acts[SHARED][b : b + 1], banks[SHARED, 1][b : b + 1], b)
-                h_grouped[b] = group_hidden(turned, 1, ring(rings, "h_pairs", 4, [P, 2 * P], F32)[:])
-            if 1 <= b <= T // P:
-                y_banks[b - 1] = second_layer(quantize(h_grouped[b - 1], P, "h"), P, w2_q[SHARED], 4 + b - 1)
-            if b >= 2:
-                cols = slice((b - 2) * P, (b - 1) * P)
-                result = keep.tile([P, P], F32, name="result%d" % (b - 2))
-                nc.vector.tensor_tensor(result[:], y_banks[b - 2][:, 0:P], routed_sum[:, cols], ADD)
-                nc.sync.dma_start(out=out[:, cols], in_=result[:])
+        w2_q[SHARED] = quantize(cast_w2(st["w2_raw"], nc.scalar.copy), N, "w2")
+        blocks = range(T // P)
+        turned = [gate_and_turn(acts[SHARED][b : b + 1], banks[SHARED, 1][b : b + 1], b) for b in blocks]
+        h_grouped = [group_hidden(turned[b], 1, ring(rings, "h_pairs", 4, [P, 2 * P], F32)[:]) for b in blocks]
+        y_banks = [second_layer(quantize(h_grouped[b], P, "h"), P, w2_q[SHARED], 4 + b) for b in blocks]
+        for b in blocks:
+            cols = slice(b * P, (b + 1) * P)
+            result = keep.tile([P, P], F32, name="result%d" % b)
+            nc.vector.tensor_tensor(result[:], y_banks[b][:, 0:P], routed_sum[:, cols], ADD)
+            nc.sync.dma_start(out=out[:, cols], in_=result[:])

@@ -21,22 +21,37 @@ P = 128
 PACK = 4
 K_PASS = P * PACK
 PASSES = K // K_PASS
-SHARED = E
 STEPS = 2 * PASSES
-TAIL_SCALAR_COLS = 256
-RAW_DEPTH = 16
-SHARES = {}
-PICK0 = 19
-PICK1 = 26
-Y_ON_V = True
-PICK_STEP = 27
-LAST_TURN = 24
-TURN_ANCHOR = True
+SHARED = E
+FIRST_SHARED = STEPS * SHARED
+LAST = FIRST_SHARED + STEPS - 1
+OFFSETS_PER_COLUMN = 16
+
+SHARED_MIDDLE_SCALAR_COLS = H // 4
+LAST_SCALAR_COLS = H // 2
+
+STAGING_TILES = 16
+CAST_TILES = 4
+CODE_TILES = 6
+SLOT_TILES = 2
+SMALL_TILES = 4
 GATE_STEP = 5
-SLOT_DEPTH = 2
-VECTOR_EXTRA = (25, 28)
-SCALAR_EXTRA = (26,)
-SHARED_ANCHOR = 27
+LIST_STEP = 8
+
+ROUTED_BANK = 4
+TURN_BANK = 0
+LAST_TURN_BANK = 5
+Y_BANK = 4
+GATE_BANK = 2
+
+
+def scalar_columns(s):
+    o = s % PASSES
+    if s == LAST:
+        return LAST_SCALAR_COLS
+    if s >= FIRST_SHARED:
+        return SHARED_MIDDLE_SCALAR_COLS if o == 1 else H
+    return 0 if o == PASSES - 1 else H
 
 
 def tile_moe_shr_glu_relu_kernel(
@@ -47,30 +62,41 @@ def tile_moe_shr_glu_relu_kernel(
         keep = ctx.enter_context(tc.tile_pool(name="keep", bufs=1))
         rings = ctx.enter_context(tc.tile_pool(name="rings", bufs=1))
         psum = ctx.enter_context(tc.psum_pool(name="psum", bufs=1))
+
         taken = {}
 
-        def ring(pool, name, depth, shape, dtype):
+        def ring(name, depth, shape, dtype):
             taken[name] = taken.get(name, 0) + 1
-            return pool.tile(shape, dtype, name="%s_%d" % (name, taken[name] % depth), align_bytes=64)
+            return rings.tile(shape, dtype, name="%s_%d" % (name, taken[name] % depth), align_bytes=64)
 
         def bank(index, shape):
             return psum.tile(shape, F32, name="bank%d" % index)
 
-        free = list(range(RAW_DEPTH))
+        free = list(range(STAGING_TILES))
         held = {}
 
-        def stage(key, width):
+        def load_rows(key, rows):
             held[key] = free[0]
             free.remove(held[key])
-            return rings.tile([P, PACK, width], F32, name="raw%d" % held[key], align_bytes=64)
+            raw = rings.tile([P, PACK, rows.shape[1]], F32, name="raw%d" % held[key], align_bytes=64)
+            nc.sync.dma_start(out=raw[:], in_=rows.rearrange("(p j) c -> p j c", j=PACK))
+            return raw
 
         def release(key):
             free.append(held[key])
 
-        first = stage(0, H)
-        nc.sync.dma_start(out=first[:], in_=w1[0, 0:K_PASS, :].rearrange("(p j) c -> p j c", j=PACK))
-        offs_sb = keep.tile([P, E * C // 16], U16, name="offs_sb")
-        nc.sync.dma_start(offs_sb[:], offs)
+        def load_pass(s):
+            o = s % PASSES
+            matrix = (w1, w3)[s // PASSES % 2]
+            return load_rows(s, matrix[s // STEPS, o * K_PASS : (o + 1) * K_PASS, :])
+
+        def load_list(offsets, name):
+            listed = keep.tile([P, offsets.shape[1]], U16, name=name)
+            nc.sync.dma_start(listed[:], offsets)
+            return listed
+
+        raws = {0: load_pass(0)}
+        offs_sb = load_list(offs, "offs_sb")
         tok_words = keep.tile([P, PASSES * T], I32, name="tok_words", align_bytes=64)
         nc.sync.dma_start(
             out=tok_words[:].rearrange("p (o t) -> p o t", o=PASSES),
@@ -85,14 +111,13 @@ def tile_moe_shr_glu_relu_kernel(
             )
         ident = keep.tile([P, P], F32, name="ident")
         make_identity(nc, ident[:])
-
         y_slots = keep.tile([P, E * C], F32, name="y_slots")
-        routed_sum = keep.tile([P, T], F32, name="routed_sum")
 
         def gather_tokens(e):
-            slots = offs_sb[:, e * C // 16 : (e + 1) * C // 16]
-            words = ring(rings, "slot_words", SLOT_DEPTH, [P, PASSES * C], U32)
-            scales = ring(rings, "slot_scales", SLOT_DEPTH, [P, C], U8)
+            columns = C // OFFSETS_PER_COLUMN
+            slots = offs_sb[:, e * columns : (e + 1) * columns]
+            words = ring("slot_words", SLOT_TILES, [P, PASSES * C], U32)
+            scales = ring("slot_scales", SLOT_TILES, [P, C], U8)
             nc.vector.tensor_copy(scales[:], tok_scales[:].indirect(slots))
             for o in range(PASSES):
                 window = tok_words[:, o * T : (o + 1) * T].bitcast(U32)
@@ -105,29 +130,27 @@ def tile_moe_shr_glu_relu_kernel(
                 in_=raw[:, :, c0:c1].rearrange("p j (c i) -> p c j i", i=4),
             )
 
-        def load_pass(s):
-            e, m, o = s // STEPS, s // PASSES % 2, s % PASSES
-            raw = stage(s, H)
-            rows = (w1, w3)[m][e, o * K_PASS : (o + 1) * K_PASS, :]
-            nc.sync.dma_start(out=raw[:], in_=rows.rearrange("(p j) c -> p j c", j=PACK))
-            return raw
-
         def cast_pass(raw, scalar_cols):
-            grouped = ring(rings, "grouped", 4, [P, PACK * H], BF16)
+            grouped = ring("grouped", CAST_TILES, [P, PACK * H], BF16)
             if scalar_cols > 0:
                 interleave(nc.scalar.copy, grouped, raw, 0, scalar_cols)
             if scalar_cols < H:
                 interleave(nc.vector.tensor_copy, grouped, raw, scalar_cols, H)
             return grouped
 
-        def multiply_pass(grouped, o, banks, words, scales):
-            width = len(banks) * P
-            w_codes = ring(rings, "w_codes", 6, [P, H], U32)
-            w_scales = ring(rings, "w_scales", 6, [P, H], U8)
-            nc.vector.quantize_mx(out=w_codes[:].bitcast(FP8X4), scales=w_scales[:], in_=grouped[:])
-            for b in range(len(banks)):
+        def quantize(grouped, width, name, depth):
+            codes = ring(name + "_codes", depth, [P, width], U32)
+            scales = ring(name + "_scales", depth, [P, width], U8)
+            nc.vector.quantize_mx(out=codes[:].bitcast(FP8X4), scales=scales[:], in_=grouped)
+            return codes, scales
+
+        def multiply_pass(grouped, o, sums, tokens):
+            words, scales = tokens
+            width = len(sums) * P
+            w_codes, w_scales = quantize(grouped[:], H, "w", CODE_TILES)
+            for b in range(len(sums)):
                 nc.tensor.matmul_mx(
-                    out=banks[b][:],
+                    out=sums[b][:],
                     lhsT=words[:, o * width + b * P : o * width + (b + 1) * P].bitcast(FP8X4),
                     lhsT_scale=scales[4 * o : P, b * P : (b + 1) * P],
                     rhs=w_codes[:].bitcast(FP8X4),
@@ -136,38 +159,26 @@ def tile_moe_shr_glu_relu_kernel(
                     stop=(o == PASSES - 1),
                 )
 
-        def by_pairs(bank):
-            return bank[:].rearrange("s (p u e) -> s u p e", u=2, e=2)
-
-        def relu_out(bank, act):
-            nc.scalar.activation(act.rearrange("s (u p e) -> s u p e", u=2, e=2), by_pairs(bank), RELU)
-
-        def load_w2(e):
-            raw = stage("w2", N)
-            nc.sync.dma_start(out=raw[:], in_=w2[e].rearrange("(p j) n -> p j n", j=PACK))
-            return raw
-
-        def cast_w2(raw, copy):
-            grouped = ring(rings, "w2_grouped", 4, [P, PACK * N], BF16)
+        def quantize_w2(raw, copy):
+            grouped = ring("w2_grouped", SMALL_TILES, [P, PACK * N], BF16)
             interleave(copy, grouped, raw, 0, N)
-            return grouped[:]
+            return quantize(grouped[:], N, "w2", SMALL_TILES)
 
-        def quantize(grouped, width, name):
-            q_codes = ring(rings, name + "_codes", 4, [P, width], U32)
-            q_scales = ring(rings, name + "_scales", 4, [P, width], U8)
-            nc.vector.quantize_mx(out=q_codes[:].bitcast(FP8X4), scales=q_scales[:], in_=grouped)
-            return q_codes, q_scales
+        def psum_by_pairs(sums):
+            return sums[:].rearrange("s (p u e) -> s u p e", u=2, e=2)
 
-        def gate_and_turn(acts, banks, turn_bank):
+        def sbuf_by_pairs(row):
+            return row.rearrange("s (u p e) -> s u p e", u=2, e=2)
+
+        def relu_into(act, sums):
+            nc.scalar.activation(act, psum_by_pairs(sums), RELU)
+            return act
+
+        def gate_and_turn(acts, sums, turn_bank):
             turned = bank(turn_bank, [P, 2, 2, P])
-            for b in range(len(banks)):
-                hidden = ring(rings, "hidden", 4, [P, H], BF16)
-                nc.vector.tensor_tensor(
-                    hidden[:].rearrange("s (u p e) -> s u p e", u=2, e=2),
-                    by_pairs(banks[b]),
-                    acts[b].rearrange("s (u p e) -> s u p e", u=2, e=2),
-                    MULT,
-                )
+            for b in range(len(sums)):
+                hidden = ring("hidden", SMALL_TILES, [P, H], BF16)
+                nc.vector.tensor_tensor(sbuf_by_pairs(hidden[:]), psum_by_pairs(sums[b]), acts[b], MULT)
                 pairs = hidden[:].bitcast(F32)
                 for u in range(2):
                     nc.tensor.transpose(turned[:, b, u, :], pairs[:, u * P : (u + 1) * P], ident[:])
@@ -180,110 +191,111 @@ def tile_moe_shr_glu_relu_kernel(
             )
             return pairs.bitcast(BF16)
 
-        def second_layer(h_q, width, w2_q, y_index):
-            h_codes, h_scales = h_q
+        def second_layer(h_mx, width, w2_mx, y_index):
             y_bank = bank(y_index, [P, C])
             nc.tensor.matmul_mx(
                 out=y_bank[:, 0:width],
-                lhsT=w2_q[0][:].bitcast(FP8X4),
-                lhsT_scale=w2_q[1][:],
-                rhs=h_codes[:].bitcast(FP8X4),
-                rhs_scale=h_scales[:],
+                lhsT=w2_mx[0][:].bitcast(FP8X4),
+                lhsT_scale=w2_mx[1][:],
+                rhs=h_mx[0][:].bitcast(FP8X4),
+                rhs_scale=h_mx[1][:],
                 start=True,
                 stop=True,
             )
             return y_bank
 
+        def store_slots(e, h_mx, w2_mx, copy):
+            copy(out=y_slots[:, e * C : (e + 1) * C], in_=second_layer(h_mx, C, w2_mx, Y_BANK)[:])
+
         def spread_gates():
             column = keep.tile([P, 2, 4], F32, name="gate_column")
             nc.sync.dma_start(out=column[:], in_=gate[:, 0, :].rearrange("r (p i) -> p r i", i=4))
-            gates = keep.tile([P, 2, T], F32, name="gates")
+            spread_sb = keep.tile([P, 2, T], F32, name="gates")
             for r in range(2):
-                spread = bank(2 + r, [P, 4, P])
+                spread = bank(GATE_BANK + r, [P, 4, P])
                 for i in range(4):
                     nc.tensor.transpose(spread[:, i, :], column[:, r, i : i + 1].to_broadcast([P, P]), ident[:])
                 nc.scalar.copy(
-                    out=gates[:, r, :].rearrange("n (p i) -> n p i", i=4),
+                    out=spread_sb[:, r, :].rearrange("n (p i) -> n p i", i=4),
                     in_=spread[:].rearrange("n i p -> n p i"),
                 )
-            return gates
+            return spread_sb
 
-        def load_list(pos, name):
-            pos_tile = keep.tile([P, T // 16], U16, name=name)
-            nc.sync.dma_start(pos_tile[:], pos)
-            return pos_tile
-
-        def pick(pos_tile, gates_row, product):
-            nc.vector.tensor_tensor(product, y_slots[:].indirect(pos_tile[:]), gates_row, MULT)
+        def pick(positions, gate_row, product):
+            nc.vector.tensor_tensor(product, y_slots[:].indirect(positions[:]), gate_row, MULT)
             return product
 
         tokens = {0: gather_tokens(0), SHARED: (tok_words, tok_scales)}
-        raws, grouped, banks, acts, w2_q, st = {}, {}, {}, {}, {}, {}
-        last = STEPS * (E + 1) - 1
+        grouped, sums, acts, w2_mx = {}, {}, {}, {}
+        for s in range(LAST + 2):
+            e, step = divmod(s, STEPS)
+            routed = e < E
+            if s <= LAST:
+                if s > 0:
+                    raws[s] = load_pass(s)
+                grouped[s] = cast_pass(raws[s], scalar_columns(s))
+            if s > 0:
+                matrix, o = divmod(s - 1, PASSES)
+                if o == 0:
+                    is_shared = matrix // 2 == SHARED
+                    blocks = (T if is_shared else C) // P
+                    first_bank = (0 if is_shared else ROUTED_BANK) + blocks * (matrix % 2)
+                    sums[matrix] = [bank(first_bank + b, [P, H]) for b in range(blocks)]
+                multiply_pass(grouped[s - 1], o, sums[matrix], tokens[matrix // 2])
 
-        def store_slots(e):
-            y_bank = second_layer(st["h_q"], C, w2_q[e], 4)
-            (nc.vector.tensor_copy if e == E - 1 and Y_ON_V else nc.scalar.copy)(out=y_slots[:, e * C : (e + 1) * C], in_=y_bank[:])
-
-        for s in range(last + 2):
-            e, k = divmod(s, STEPS)
-            if s <= last:
-                raws[s] = first if s == 0 else load_pass(s)
-                on_vector = (s % PASSES == PASSES - 1 or s in VECTOR_EXTRA) and s not in SCALAR_EXTRA
-                share = SHARES.get(s, TAIL_SCALAR_COLS if s == last else (0 if on_vector else H))
-                grouped[s] = cast_pass(raws[s], share)
-            if s >= 1:
-                pe, pm, po = (s - 1) // STEPS, (s - 1) // PASSES % 2, (s - 1) % PASSES
-                if po == 0:
-                    blocks = (T if pe == SHARED else C) // P
-                    base = 4 * pm if pe == SHARED else 4 + 2 * pm
-                    banks[pe, pm] = [bank(base + b, [P, H]) for b in range(blocks)]
-                multiply_pass(grouped[s - 1], po, banks[pe, pm], tokens[pe][0], tokens[pe][1])
-            if k == 0 and 1 <= e <= E:
-                st["turned"] = gate_and_turn(acts[e - 1], banks[e - 1, 1], 0 if e < E else 5)
-                if e < E:
+            if step == 0 and 0 < e <= E:
+                turned = gate_and_turn(acts[e - 1], sums[2 * e - 1], TURN_BANK if routed else LAST_TURN_BANK)
+                if routed:
                     tokens[e] = gather_tokens(e)
-            if (k == 1 and 1 <= e < E) or s == LAST_TURN:
-                st["h_q"] = quantize(group_hidden(st["turned"], C // P, raws[s if TURN_ANCHOR or e < E else 13][:, 0, :]), C, "h")
-                if e == E:
-                    store_slots(e - 1)
-            if k == 3 and e < E:
-                st["w2_raw"] = load_w2(e)
-            if k == 4 and e < E:
-                w2_q[e] = quantize(cast_w2(st["w2_raw"], nc.vector.tensor_copy), N, "w2")
+            if (step == 1 and 0 < e < E) or s == FIRST_SHARED:
+                h_mx = quantize(group_hidden(turned, C // P, raws[s][:, 0, :]), C, "h", SMALL_TILES)
+            if s == FIRST_SHARED:
+                store_slots(E - 1, h_mx, w2_mx[E - 1], nc.vector.tensor_copy)
+            if step == PASSES and routed:
+                w2_raw = load_rows("w2", w2[e])
+            if step == PASSES + 1 and routed:
+                w2_mx[e] = quantize_w2(w2_raw, nc.vector.tensor_copy)
                 release("w2")
                 release(s - 1)
-                acts[e] = [raws[s - 1 if s in VECTOR_EXTRA else s][:, b, :] for b in range(C // P)]
-                for b in range(C // P):
-                    relu_out(banks[e, 0][b], acts[e][b])
-                if e >= 1:
-                    store_slots(e - 1)
-            if s == max(SHARED_ANCHOR, 27):
-                home = raws[SHARED_ANCHOR] if SHARED_ANCHOR >= 0 else raws[7]
-                acts[e] = [home[:, b, :] for b in range(T // P)]
-                for b in range(T // P):
-                    relu_out(banks[e, 0][b], acts[e][b])
+                acts[e] = [relu_into(sbuf_by_pairs(raws[s][:, b, :]), sums[2 * e][b]) for b in range(C // P)]
+                if e > 0:
+                    store_slots(e - 1, h_mx, w2_mx[e - 1], nc.scalar.copy)
+
             if s == GATE_STEP:
                 gates = spread_gates()
-            if s == 8:
-                pos_sb = [load_list(pos1, "pos1_sb"), load_list(pos2, "pos2_sb")]
-            if s <= last and not (e < E and (k in (3, 4) or (k == 1 and e >= 1))):
-                release(s)
-            if s == PICK_STEP:
-                picked = [pick(pos_sb[0], gates[:, 0, :], raws[PICK0][:, 1, :])]
-            if s == PICK_STEP:
-                picked.append(pick(pos_sb[1], gates[:, 1, :], raws[PICK1][:, 2, :]))
-                nc.vector.tensor_tensor(routed_sum[:], picked[0], picked[1], ADD)
-            if s == last:
-                st["w2_raw"] = load_w2(SHARED)
+            if s == LIST_STEP:
+                pos1_sb = load_list(pos1, "pos1_sb")
+                pos2_sb = load_list(pos2, "pos2_sb")
 
-        w2_q[SHARED] = quantize(cast_w2(st["w2_raw"], nc.scalar.copy), N, "w2")
-        blocks = range(T // P)
-        turned = [gate_and_turn(acts[SHARED][b : b + 1], banks[SHARED, 1][b : b + 1], b) for b in blocks]
-        h_grouped = [group_hidden(turned[b], 1, ring(rings, "h_pairs", 4, [P, 2 * P], F32)[:]) for b in blocks]
-        y_banks = [second_layer(quantize(h_grouped[b], P, "h"), P, w2_q[SHARED], 4 + b) for b in blocks]
-        for b in blocks:
+            if s == FIRST_SHARED + PASSES:
+                acts[e] = [relu_into(sbuf_by_pairs(raws[s][:, b, :]), sums[2 * e][b]) for b in range(2)]
+                picked1 = pick(pos1_sb, gates[:, 0, :], raws[FIRST_SHARED - STEPS + 1][:, 1, :])
+                picked2 = pick(pos2_sb, gates[:, 1, :], raws[s - 1][:, 2, :])
+            if s == LAST:
+                for b in range(2):
+                    half = raws[s][:, 2 * b : 2 * b + 2, 0:LAST_SCALAR_COLS]
+                    acts[e].append(relu_into(half.rearrange("s u (p e) -> s u p e", e=2), sums[2 * e][2 + b]))
+                w2_raw = load_rows("w2", w2[SHARED])
+
+            if routed and step not in (PASSES, PASSES + 1) and not (step == 1 and e > 0):
+                release(s)
+
+        routed_sum = grouped[LAST][:, 0 : 2 * T].bitcast(F32)
+        nc.vector.tensor_tensor(routed_sum, picked1, picked2, ADD)
+        w2_mx[SHARED] = quantize_w2(w2_raw, nc.scalar.copy)
+
+        token_blocks = range(T // P)
+        other_factor = sums[2 * SHARED + 1]
+        turned_blocks = [gate_and_turn(acts[SHARED][b : b + 1], other_factor[b : b + 1], b) for b in token_blocks]
+        h_blocks = [
+            group_hidden(turned_blocks[b], 1, ring("h_pairs", SMALL_TILES, [P, 2 * P], F32)[:]) for b in token_blocks
+        ]
+        y_blocks = [
+            second_layer(quantize(h_blocks[b], P, "h", SMALL_TILES), P, w2_mx[SHARED], T // P + b)
+            for b in token_blocks
+        ]
+        for b in token_blocks:
             cols = slice(b * P, (b + 1) * P)
             result = keep.tile([P, P], F32, name="result%d" % b)
-            nc.vector.tensor_tensor(result[:], y_banks[b][:, 0:P], routed_sum[:, cols], ADD)
+            nc.vector.tensor_tensor(result[:], y_blocks[b][:, 0:P], routed_sum[:, cols], ADD)
             nc.sync.dma_start(out=out[:, cols], in_=result[:])

from contextlib import ExitStack

import concourse.mybir as mybir
from concourse.masks import make_identity

K, T, E, C, H, N = 1536, 512, 4, 256, 512, 128
FLOPS = 2 * (E * C + T) * H * (2 * K + N)

F32 = mybir.dt.float32
BF16 = mybir.dt.bfloat16
I32 = mybir.dt.int32
U32 = mybir.dt.uint32
U16 = mybir.dt.uint16
U8 = mybir.dt.uint8
FP8X4 = mybir.dt.float8_e4m3fn_x4
MULT = mybir.AluOpType.mult
ADD = mybir.AluOpType.add
RELU = mybir.ActivationFunctionType.Relu

P = 128
PACK = 4
K_PASS = P * PACK
PASSES = K // K_PASS
STEPS = 2 * PASSES
SHARED = E
FIRST_SHARED = STEPS * SHARED
LAST = FIRST_SHARED + STEPS - 1
OFFSETS_PER_COLUMN = 16

SHARED_MIDDLE_SCALAR_COLS = H // 4
LAST_SCALAR_COLS = H // 2

STAGING_TILES = 16
CAST_TILES = 4
CODE_TILES = 6
SLOT_TILES = 2
SMALL_TILES = 4
GATE_STEP = 5
LIST_STEP = 8

ROUTED_BANK = 4
TURN_BANK = 0
LAST_TURN_BANK = 5
Y_BANK = 4
GATE_BANK = 2


def scalar_columns(s):
    o = s % PASSES
    if s == LAST:
        return LAST_SCALAR_COLS
    if s >= FIRST_SHARED:
        return SHARED_MIDDLE_SCALAR_COLS if o == 1 else H
    return 0 if o == PASSES - 1 else H


def tile_moe_shr_glu_relu_kernel(
    tc, x_words, x_scales, w1, w3, w2, gate, offs, pos1, pos2, out
):
    nc = tc.nc
    with ExitStack() as ctx:
        keep = ctx.enter_context(tc.tile_pool(name="keep", bufs=1))
        rings = ctx.enter_context(tc.tile_pool(name="rings", bufs=1))
        psum = ctx.enter_context(tc.psum_pool(name="psum", bufs=1))

        taken = {}

        def ring(name, depth, shape, dtype):
            taken[name] = taken.get(name, 0) + 1
            return rings.tile(shape, dtype, name="%s_%d" % (name, taken[name] % depth), align_bytes=64)

        def bank(index, shape):
            return psum.tile(shape, F32, name="bank%d" % index)

        free = list(range(STAGING_TILES))
        held = {}

        def load_rows(key, rows):
            held[key] = free[0]
            free.remove(held[key])
            raw = rings.tile([P, PACK, rows.shape[1]], F32, name="raw%d" % held[key], align_bytes=64)
            nc.sync.dma_start(out=raw[:], in_=rows.rearrange("(p j) c -> p j c", j=PACK))
            return raw

        def release(key):
            free.append(held[key])

        def load_pass(s):
            o = s % PASSES
            matrix = (w1, w3)[s // PASSES % 2]
            return load_rows(s, matrix[s // STEPS, o * K_PASS : (o + 1) * K_PASS, :])

        def load_list(offsets, name):
            listed = keep.tile([P, offsets.shape[1]], U16, name=name)
            nc.sync.dma_start(listed[:], offsets)
            return listed

        raws = {0: load_pass(0)}
        offs_sb = load_list(offs, "offs_sb")
        tok_words = keep.tile([P, PASSES * T], I32, name="tok_words", align_bytes=64)
        nc.sync.dma_start(
            out=tok_words[:].rearrange("p (o t) -> p o t", o=PASSES),
            in_=x_words.rearrange("o p t r -> p o (t r)").bitcast(I32),
        )
        tok_scales = keep.tile([P, T], U8, name="tok_scales", align_bytes=64)
        nc.gpsimd.memset(tok_scales[:].bitcast(I32), 0)
        for q in range(4):
            nc.sync.dma_start(
                out=tok_scales[32 * q : 32 * q + 4 * PASSES, :].bitcast(I32),
                in_=x_scales[:, 4 * q : 4 * q + 4, :].bitcast(I32),
            )
        ident = keep.tile([P, P], F32, name="ident")
        make_identity(nc, ident[:])
        y_slots = keep.tile([P, E * C], F32, name="y_slots")

        def gather_tokens(e):
            columns = C // OFFSETS_PER_COLUMN
            slots = offs_sb[:, e * columns : (e + 1) * columns]
            words = ring("slot_words", SLOT_TILES, [P, PASSES * C], U32)
            scales = ring("slot_scales", SLOT_TILES, [P, C], U8)
            nc.vector.tensor_copy(scales[:], tok_scales[:].indirect(slots))
            for o in range(PASSES):
                window = tok_words[:, o * T : (o + 1) * T].bitcast(U32)
                nc.vector.tensor_copy(words[:, o * C : (o + 1) * C], window.indirect(slots))
            return words, scales

        def interleave(copy, grouped, raw, c0, c1):
            copy(
                out=grouped[:, PACK * c0 : PACK * c1].rearrange("p (c i j) -> p c j i", i=4, j=PACK),
                in_=raw[:, :, c0:c1].rearrange("p j (c i) -> p c j i", i=4),
            )

        def cast_pass(raw, scalar_cols):
            grouped = ring("grouped", CAST_TILES, [P, PACK * H], BF16)
            if scalar_cols > 0:
                interleave(nc.scalar.copy, grouped, raw, 0, scalar_cols)
            if scalar_cols < H:
                interleave(nc.vector.tensor_copy, grouped, raw, scalar_cols, H)
            return grouped

        def quantize(grouped, width, name, depth):
            codes = ring(name + "_codes", depth, [P, width], U32)
            scales = ring(name + "_scales", depth, [P, width], U8)
            nc.vector.quantize_mx(out=codes[:].bitcast(FP8X4), scales=scales[:], in_=grouped)
            return codes, scales

        def multiply_pass(grouped, o, sums, tokens):
            words, scales = tokens
            width = len(sums) * P
            w_codes, w_scales = quantize(grouped[:], H, "w", CODE_TILES)
            for b in range(len(sums)):
                nc.tensor.matmul_mx(
                    out=sums[b][:],
                    lhsT=words[:, o * width + b * P : o * width + (b + 1) * P].bitcast(FP8X4),
                    lhsT_scale=scales[4 * o : P, b * P : (b + 1) * P],
                    rhs=w_codes[:].bitcast(FP8X4),
                    rhs_scale=w_scales[:],
                    start=(o == 0),
                    stop=(o == PASSES - 1),
                )

        def quantize_w2(raw, copy):
            grouped = ring("w2_grouped", SMALL_TILES, [P, PACK * N], BF16)
            interleave(copy, grouped, raw, 0, N)
            return quantize(grouped[:], N, "w2", SMALL_TILES)

        def psum_by_pairs(sums):
            return sums[:].rearrange("s (p u e) -> s u p e", u=2, e=2)

        def sbuf_by_pairs(row):
            return row.rearrange("s (u p e) -> s u p e", u=2, e=2)

        def relu_into(act, sums):
            nc.scalar.activation(act, psum_by_pairs(sums), RELU)
            return act

        def gate_and_turn(acts, sums, turn_bank):
            turned = bank(turn_bank, [P, 2, 2, P])
            for b in range(len(sums)):
                hidden = ring("hidden", SMALL_TILES, [P, H], BF16)
                nc.vector.tensor_tensor(sbuf_by_pairs(hidden[:]), psum_by_pairs(sums[b]), acts[b], MULT)
                pairs = hidden[:].bitcast(F32)
                for u in range(2):
                    nc.tensor.transpose(turned[:, b, u, :], pairs[:, u * P : (u + 1) * P], ident[:])
            return turned

        def group_hidden(turned, blocks, pairs):
            nc.scalar.copy(
                out=pairs.rearrange("p (b s u) -> p b s u", s=P, u=2),
                in_=turned[:, 0:blocks, :, :].rearrange("p b u s -> p b s u"),
            )
            return pairs.bitcast(BF16)

        def second_layer(h_mx, width, w2_mx, y_index):
            y_bank = bank(y_index, [P, C])
            nc.tensor.matmul_mx(
                out=y_bank[:, 0:width],
                lhsT=w2_mx[0][:].bitcast(FP8X4),
                lhsT_scale=w2_mx[1][:],
                rhs=h_mx[0][:].bitcast(FP8X4),
                rhs_scale=h_mx[1][:],
                start=True,
                stop=True,
            )
            return y_bank

        def store_slots(e, h_mx, w2_mx, copy):
            copy(out=y_slots[:, e * C : (e + 1) * C], in_=second_layer(h_mx, C, w2_mx, Y_BANK)[:])

        def spread_gates():
            column = keep.tile([P, 2, 4], F32, name="gate_column")
            nc.sync.dma_start(out=column[:], in_=gate[:, 0, :].rearrange("r (p i) -> p r i", i=4))
            spread_sb = keep.tile([P, 2, T], F32, name="gates")
            for r in range(2):
                spread = bank(GATE_BANK + r, [P, 4, P])
                for i in range(4):
                    nc.tensor.transpose(spread[:, i, :], column[:, r, i : i + 1].to_broadcast([P, P]), ident[:])
                nc.scalar.copy(
                    out=spread_sb[:, r, :].rearrange("n (p i) -> n p i", i=4),
                    in_=spread[:].rearrange("n i p -> n p i"),
                )
            return spread_sb

        def pick(positions, gate_row, product):
            nc.vector.tensor_tensor(product, y_slots[:].indirect(positions[:]), gate_row, MULT)
            return product

        tokens = {0: gather_tokens(0), SHARED: (tok_words, tok_scales)}
        grouped, sums, acts, w2_mx = {}, {}, {}, {}
        for s in range(LAST + 2):
            e, step = divmod(s, STEPS)
            routed = e < E
            if s <= LAST:
                if s > 0:
                    raws[s] = load_pass(s)
                grouped[s] = cast_pass(raws[s], scalar_columns(s))
            if s > 0:
                matrix, o = divmod(s - 1, PASSES)
                if o == 0:
                    is_shared = matrix // 2 == SHARED
                    blocks = (T if is_shared else C) // P
                    first_bank = (0 if is_shared else ROUTED_BANK) + blocks * (matrix % 2)
                    sums[matrix] = [bank(first_bank + b, [P, H]) for b in range(blocks)]
                multiply_pass(grouped[s - 1], o, sums[matrix], tokens[matrix // 2])

            if step == 0 and 0 < e <= E:
                turned = gate_and_turn(acts[e - 1], sums[2 * e - 1], TURN_BANK if routed else LAST_TURN_BANK)
                if routed:
                    tokens[e] = gather_tokens(e)
            if (step == 1 and 0 < e < E) or s == FIRST_SHARED:
                h_mx = quantize(group_hidden(turned, C // P, raws[s][:, 0, :]), C, "h", SMALL_TILES)
            if s == FIRST_SHARED:
                store_slots(E - 1, h_mx, w2_mx[E - 1], nc.vector.tensor_copy)
            if step == PASSES and routed:
                w2_raw = load_rows("w2", w2[e])
            if step == PASSES + 1 and routed:
                w2_mx[e] = quantize_w2(w2_raw, nc.vector.tensor_copy)
                release("w2")
                release(s - 1)
                acts[e] = [relu_into(sbuf_by_pairs(raws[s][:, b, :]), sums[2 * e][b]) for b in range(C // P)]
                if e > 0:
                    store_slots(e - 1, h_mx, w2_mx[e - 1], nc.scalar.copy)

            if s == GATE_STEP:
                gates = spread_gates()
            if s == LIST_STEP:
                pos1_sb = load_list(pos1, "pos1_sb")
                pos2_sb = load_list(pos2, "pos2_sb")

            if s == FIRST_SHARED + PASSES:
                acts[e] = [relu_into(sbuf_by_pairs(raws[s][:, b, :]), sums[2 * e][b]) for b in range(2)]
                picked1 = pick(pos1_sb, gates[:, 0, :], raws[FIRST_SHARED - STEPS + 1][:, 1, :])
                picked2 = pick(pos2_sb, gates[:, 1, :], raws[s - 1][:, 2, :])
            if s == LAST:
                for b in range(2):
                    half = raws[s][:, 2 * b : 2 * b + 2, 0:LAST_SCALAR_COLS]
                    acts[e].append(relu_into(half.rearrange("s u (p e) -> s u p e", e=2), sums[2 * e][2 + b]))
                w2_raw = load_rows("w2", w2[SHARED])

            if routed and step not in (PASSES, PASSES + 1) and not (step == 1 and e > 0):
                release(s)

        routed_sum = grouped[LAST][:, 0 : 2 * T].bitcast(F32)
        nc.vector.tensor_tensor(routed_sum, picked1, picked2, ADD)
        w2_mx[SHARED] = quantize_w2(w2_raw, nc.scalar.copy)

        token_blocks = range(T // P)
        other_factor = sums[2 * SHARED + 1]
        turned_blocks = [gate_and_turn(acts[SHARED][b : b + 1], other_factor[b : b + 1], b) for b in token_blocks]
        h_blocks = [
            group_hidden(turned_blocks[b], 1, ring("h_pairs", SMALL_TILES, [P, 2 * P], F32)[:]) for b in token_blocks
        ]
        y_blocks = [
            second_layer(quantize(h_blocks[b], P, "h", SMALL_TILES), P, w2_mx[SHARED], T // P + b)
            for b in token_blocks
        ]
        for b in token_blocks:
            cols = slice(b * P, (b + 1) * P)
            result = keep.tile([P, P], F32, name="result%d" % b)
            nc.vector.tensor_tensor(result[:], y_blocks[b][:, 0:P], routed_sum[:, cols], ADD)
            nc.sync.dma_start(out=out[:, cols], in_=result[:])
